import numpy as np
import ml_dtypes


def mxq(x, axis, fmt="e4m3"):
    dtype, down = {"e4m3": (ml_dtypes.float8_e4m3fn, 7), "e5m2": (ml_dtypes.float8_e5m2, 14)}[fmt]
    v = np.moveaxis(np.asarray(x, np.float32).astype(ml_dtypes.bfloat16).astype(np.float64), axis, -1)
    blocks = v.reshape(v.shape[:-1] + (-1, 32))
    amax = np.abs(blocks).max(-1, keepdims=True)
    byte = np.maximum(np.where(amax > 0, np.frexp(amax)[1] - 1 + 127, 0) - down, 1)
    scale = np.exp2(byte - 127.0)
    codes = (blocks / scale).astype(np.float32).astype(dtype).astype(np.float64)
    return np.moveaxis((codes * scale).reshape(v.shape), -1, axis)


WIDE = False


def mx_kscale(k):
    if not WIDE:
        return np.ones(k)
    levels = np.array([10, -10, 5, -5, 0])
    if k % 512:
        return np.exp2(np.random.permutation(np.resize(levels, k // 32))).repeat(32)
    a = np.empty((k // 512, 16))
    for p in range(k // 512):
        a[p, :8] = np.random.permutation(np.resize(levels, 8))
        for g in range(8):
            far = levels[np.abs(levels - a[p, g]) >= 10]
            a[p, g + 8] = far[np.random.randint(len(far))]
    return np.exp2(a.ravel()).repeat(32)


def f64(x):
    return np.asarray(x).astype(np.float64)


def striped(idx):
    return np.tile(idx.reshape(-1, 16).T, (8, 1)).astype(np.uint16)


def unstriped(offs):
    return offs[:16].T.reshape(-1).astype(np.int64)


E2M1 = np.array([0.0, 0.5, 1.0, 1.5, 2.0, 3.0, 4.0, 6.0, -0.0, -0.5, -1.0, -1.5, -2.0, -3.0, -4.0, -6.0])


def pack_weight(w, fmt):
    k, n = w.shape
    w = f64(np.asarray(w, np.float32).astype(ml_dtypes.bfloat16)).reshape(k // 32, 32, n)
    amax = np.abs(w).max(1)
    if fmt == "e4m3":
        byte = np.frexp(amax)[1] - 1 + 127 - 7
    else:
        mant, ex = np.frexp(amax / 6.0)
        byte = np.where(mant > 0.5, ex, ex - 1) + 127
    byte = np.clip(np.where(amax > 0, byte, 1), 1, 254)
    scaled = (w * np.exp2(127.0 - byte)[:, None, :]).reshape(k, n).astype(np.float32)
    by_word = np.ascontiguousarray(scaled.reshape(k // 512, 128, 4, n).transpose(0, 1, 3, 2))
    if fmt == "e4m3":
        words = by_word.astype(ml_dtypes.float8_e4m3fn).view(np.uint8)
    else:
        c = by_word.astype(ml_dtypes.float4_e2m1fn).view(np.uint8) & 0xF
        words = (c[..., 0::2] | (c[..., 1::2] << 4)).reshape(k // 512, 128, 2 * n)
    return np.ascontiguousarray(words), np.ascontiguousarray(byte.astype(np.uint8).reshape(k // 512, 16, n))


def unpack_weight(words, scales, fmt):
    g, _, n = scales.shape
    words = np.ascontiguousarray(words).reshape(g, 128, n, -1)
    if fmt == "e4m3":
        vals = words.view(ml_dtypes.float8_e4m3fn).astype(np.float64)
    else:
        nib = np.empty((g, 128, n, 4), np.uint8)
        nib[..., 0::2] = words & 0xF
        nib[..., 1::2] = words >> 4
        vals = E2M1[nib]
    vals = vals * np.repeat(np.exp2(scales.astype(np.float64) - 127.0), 8, axis=1)[..., None]
    return vals.transpose(0, 1, 3, 2).reshape(g * 512, n)


def gelu(v):
    return 0.5 * v * (1.0 + np.tanh(np.sqrt(2.0 / np.pi) * (v + 0.044715 * v**3)))


K, H, N, T, S, P = 1536, 1024, 768, 4096, 1024, 512


def setup_inputs():
    n = np.random.standard_normal
    s = mx_kscale(K)[:, None]
    u = mx_kscale(H)[:, None]
    d = {}
    d["tab_words"], d["tab_scales"] = pack_weight(n((K, T)) * s, "e2m1")
    d["offs"] = striped(np.random.permutation(T)[:S])
    d["pos1"] = striped(np.random.permutation(S)[:P])
    d["pos2"] = striped(np.random.permutation(S)[:P])
    d["w1"] = (1.2 * n((K, H)) / K ** 0.5 / s).astype(np.float32)
    d["gain"] = (np.exp(0.3 * n(H)) * u[:, 0]).astype(np.float32)
    d["w4_words"], d["w4_scales"] = pack_weight(n((H, N)) / H ** 0.5 / u, "e2m1")
    d["mix"] = np.exp(0.4 * n((N, P))).astype(np.float32)
    return d


def reference(tab_words, tab_scales, offs, pos1, pos2, w1, gain, w4_words, w4_scales, mix):
    v = unpack_weight(tab_words, tab_scales, "e2m1")[:, unstriped(offs)]
    h = mxq(f64(w1), 0, "e4m3").T @ v
    calc = h[:, unstriped(pos1)]
    sint = h[:, unstriped(pos2)]
    z = f64(gain)[:, None] * (np.log(1.0 + np.square(calc)) - sint)
    w4 = unpack_weight(w4_words, w4_scales, "e2m1")
    y = w4.T @ mxq(z, 0, "e4m3")
    act = y / (1.0 + np.exp(-y))
    return act * f64(mix)

@@ -1,0 +1,300 @@
+from contextlib import ExitStack
+
+import concourse.mybir as mybir
+
+K, H, N, T, S, M = 1536, 1024, 768, 4096, 1024, 512
+FLOPS = 2 * K * H * S + 2 * H * N * M
+
+F32 = mybir.dt.float32
+BF16 = mybir.dt.bfloat16
+I32 = mybir.dt.int32
+U32 = mybir.dt.uint32
+U16 = mybir.dt.uint16
+U8 = mybir.dt.uint8
+FP8X4 = mybir.dt.float8_e4m3fn_x4
+FP4X4 = mybir.dt.float4_e2m1fn_x4
+ACT = mybir.ActivationFunctionType
+ALU = mybir.AluOpType
+
+P = 128
+KP = K // 512
+HP = H // 512
+BANK = 512
+SPLIT = 44
+
+
+def tile_list_kiln_zone_scores_kernel(tc, tab_words, tab_scales, offs, pos1, pos2, w1, gain, w4_words, w4_scales, mix, out):
+    nc = tc.nc
+    with ExitStack() as ctx:
+        keep = ctx.enter_context(tc.tile_pool(name="keep", bufs=1))
+        ring = ctx.enter_context(tc.tile_pool(name="ring", bufs=3))
+        psum = ctx.enter_context(tc.psum_pool(name="psum", bufs=1))
+
+        offs_sb = keep.tile([P, S // 16], U16, name="offs_sb")
+        pos1_sb = keep.tile([P, M // 16], U16, name="pos1_sb")
+        pos2_sb = keep.tile([P, M // 16], U16, name="pos2_sb")
+        tab_w = [keep.tile([P, T], U16, name="tab_w%d" % a, tag="tab%d" % a, align_bytes=64) for a in range(KP)]
+        tab_s = keep.tile([P, T], U8, name="tab_s", tag="scales", align_bytes=64)
+        v_w = [keep.tile([P, S], U16, name="v_w%d" % a, align_bytes=64) for a in range(KP)]
+        v_s = [keep.tile([P, S], U8, name="v_s%d" % a, align_bytes=64) for a in range(KP)]
+        gain_sb = [keep.tile([P, 4], F32, name="gain_sb%d" % b) for b in range(HP)]
+        ngain = keep.tile([P, HP, 4], F32, name="ngain")
+        w1_c = {}
+        w1_s = {}
+        w1_raw = {}
+
+        nc.vector.memset(tab_s[:].bitcast(I32), 0)
+        for a in range(1, KP):
+            nc.vector.memset(v_s[a][96:128, :].bitcast(I32), 0)
+
+        def load_tab(a, parts):
+            w = T // 2 // parts
+            for i in range(parts):
+                nc.sync.dma_start(out=tab_w[a][:].bitcast(I32)[:, i * w : (i + 1) * w], in_=tab_words[a].bitcast(I32)[:, i * w : (i + 1) * w])
+
+        def load_w1(a, b, tag):
+            raw = keep.tile([P, 2, 4, 256], F32, name="w1_raw%d%d" % (a, b), tag=tag, align_bytes=64)
+            for u in range(2):
+                rows = w1[512 * a : 512 * (a + 1), 512 * b + 256 * u : 512 * b + 256 * (u + 1)]
+                nc.sync.dma_start(out=raw[:, u], in_=rows.rearrange("(p j) c -> p j c", j=4))
+            w1_raw[(a, b)] = raw
+
+        gain_v = gain.rearrange("(b p t) -> b p t", b=HP, t=4)
+        nc.sync.dma_start(offs_sb[:], offs)
+        nc.sync.dma_start(pos1_sb[:], pos1)
+        nc.sync.dma_start(pos2_sb[:], pos2)
+        nc.sync.dma_start(out=gain_sb[0][:], in_=gain_v[0])
+        load_tab(0, 2)
+        load_w1(0, 0, "raw0")
+        nc.sync.dma_start(out=gain_sb[1][:], in_=gain_v[1])
+        for q in range(4):
+            (nc.scalar if q < 2 else nc.sync).dma_start(
+                out=tab_s[32 * q : 32 * q + 4 * KP, :].bitcast(I32),
+                in_=tab_scales[:, 4 * q : 4 * q + 4, :].bitcast(I32),
+            )
+        load_tab(1, 1)
+        load_w1(1, 0, "raw1")
+        load_tab(2, 1)
+
+        def gather_words(a):
+            nc.vector.tensor_copy(v_w[a][:], tab_w[a][:].indirect(offs_sb[:]))
+
+        def gather_scales():
+            nc.vector.tensor_copy(v_s[0][:], tab_s[:].indirect(offs_sb[:]))
+            for a in range(1, KP):
+                nc.sync.dma_start(
+                    out=v_s[a][0:100, :].bitcast(I32),
+                    in_=v_s[0][4 * a : 4 * a + 100, :].bitcast(I32),
+                )
+
+        def cast_w1(copy, w_bf, a, b, m0, m1):
+            u = m0 // 64
+            src = w1_raw[(a, b)][:, u].rearrange("p j (m t) -> p m j t", t=4)[:, m0 - 64 * u : m1 - 64 * u]
+            dst = w_bf[:].rearrange("p t m j -> p m j t")[:, m0:m1]
+            copy(dst, src)
+
+        def quant_w1(a, b, w_bf, parts):
+            w1_c[(a, b)] = keep.tile([P, 512], U32, name="w1_c%d%d" % (a, b), align_bytes=64)
+            w1_s[(a, b)] = keep.tile([P, 512], U8, name="w1_s%d%d" % (a, b), align_bytes=64)
+            flat = w_bf[:].rearrange("p t m j -> p (t m j)")
+            w = 512 // parts
+            for i in range(parts):
+                nc.vector.quantize_mx(
+                    out=w1_c[(a, b)][:, i * w : (i + 1) * w].bitcast(FP8X4),
+                    scales=w1_s[(a, b)][:, i * w : (i + 1) * w],
+                    in_=flat[:, 4 * i * w : 4 * (i + 1) * w],
+                )
+
+        def new_bf(a, b, tag):
+            return keep.tile([P, 4, P, 4], BF16, name="w_bf%d%d" % (a, b), tag=tag, align_bytes=64)
+
+        banks = {}
+
+        def stage1_pass(a, b, t):
+            for half in range(2):
+                if a == 0:
+                    banks[(t, half)] = psum.tile([P, BANK], F32, name="bank%d%d" % (t, half))
+                cols = slice(half * BANK, (half + 1) * BANK)
+                nc.tensor.matmul_mx(
+                    out=banks[(t, half)][:],
+                    lhsT=w1_c[(a, b)][:, t * P : (t + 1) * P].bitcast(FP8X4),
+                    lhsT_scale=w1_s[(a, b)][:, t * P : (t + 1) * P],
+                    rhs=v_w[a][:, cols].bitcast(FP4X4),
+                    rhs_scale=v_s[a][:, cols],
+                    start=(a == 0),
+                    stop=(a == KP - 1),
+                )
+
+        gather_words(0)
+        gather_scales()
+        load_w1(2, 0, "scales")
+        w_bf = new_bf(0, 0, "bf0")
+        cast_w1(nc.scalar.copy, w_bf, 0, 0, 0, 64)
+        cast_w1(nc.scalar.copy, w_bf, 0, 0, 64, 128)
+        quant_w1(0, 0, w_bf, 1)
+        for t in range(4):
+            stage1_pass(0, 0, t)
+        gather_words(1)
+        w_bf = new_bf(1, 0, "bf1")
+        cast_w1(nc.scalar.copy, w_bf, 1, 0, 0, 64)
+        cast_w1(nc.scalar.copy, w_bf, 1, 0, 64, 128)
+        quant_w1(1, 0, w_bf, 1)
+        gather_words(2)
+        w_bf = new_bf(2, 0, "bf2")
+        cast_w1(nc.scalar.copy, w_bf, 2, 0, 0, 64)
+        cast_w1(nc.vector.tensor_copy, w_bf, 2, 0, 64, 64 + SPLIT)
+        cast_w1(nc.scalar.copy, w_bf, 2, 0, 64 + SPLIT, 128)
+        quant_w1(2, 0, w_bf, 4)
+        for t in range(4):
+            stage1_pass(1, 0, t)
+            stage1_pass(2, 0, t)
+        load_w1(0, 1, "tab1")
+        load_w1(1, 1, "raw1")
+        load_w1(2, 1, "tab2")
+        for b in range(HP):
+            nc.vector.tensor_scalar(ngain[:, b, :], gain_sb[b][:], -1.0, None, ALU.mult)
+
+        h = {}
+        logs = {}
+
+        def evacuate(b, t, first_copy):
+            h[(b, t)] = keep.tile([P, S], F32, name="h%d%d" % (b, t))
+            first_copy(h[(b, t)][:, 0:BANK], banks[(t, 0)][:])
+            nc.scalar.copy(h[(b, t)][:, BANK:S], banks[(t, 1)][:])
+
+        def log_term(b, t, tag):
+            calc = keep.tile([P, M], F32, name="calc%d%d" % (b, t), tag=tag, align_bytes=64)
+            nc.vector.tensor_copy(calc[:], h[(b, t)][:].indirect(pos1_sb[:]))
+            logs[(b, t)] = keep.tile([P, M], F32, name="log%d%d" % (b, t))
+            nc.scalar.activation(logs[(b, t)][:], calc[:], ACT.Square)
+            nc.scalar.activation(logs[(b, t)][:], logs[(b, t)][:], ACT.Ln, bias=1.0)
+
+        def difference(dst, b, t, m0, m1):
+            nc.vector.tensor_tensor(
+                dst, h[(b, t)][:].indirect(pos2_sb[:, m0 // 16 : m1 // 16]), logs[(b, t)][:, m0:m1], ALU.subtract
+            )
+
+        def scale_z(diff, b, width, name, tag):
+            z_bf = keep.tile([P, width, 4], BF16, name="z_bf" + name, tag=tag, align_bytes=64)
+            nc.vector.tensor_tensor(
+                z_bf[:].rearrange("p (c i) t -> p c t i", i=4),
+                diff.rearrange("p t (c i) -> p c t i", i=4),
+                ngain[:, b, :].unsqueeze(1).unsqueeze(3).to_broadcast([P, width // 4, 4, 4]),
+                ALU.mult,
+            )
+            return z_bf
+
+        def quant_z(z_bf, width, name):
+            z_c = keep.tile([P, width], U32, name="z_c" + name, align_bytes=64)
+            z_s = keep.tile([P, width], U8, name="z_s" + name, align_bytes=64)
+            nc.vector.quantize_mx(out=z_c[:].bitcast(FP8X4), scales=z_s[:], in_=z_bf[:].rearrange("p m t -> p (m t)"))
+            return z_c, z_s
+
+        diff0 = keep.tile([P, 4, M], F32, name="diff0")
+        evacuate(0, 0, nc.vector.tensor_copy)
+        evacuate(0, 1, nc.scalar.copy)
+        log_term(0, 0, "late")
+        evacuate(0, 2, nc.scalar.copy)
+        log_term(0, 1, "calc1")
+        difference(diff0[:, 0, :], 0, 0, 0, M)
+        evacuate(0, 3, nc.scalar.copy)
+        bf01 = new_bf(0, 1, "late")
+        cast_w1(nc.scalar.copy, bf01, 0, 1, 0, 64)
+        log_term(0, 2, "calc2")
+        difference(diff0[:, 1, :], 0, 1, 0, M)
+        cast_w1(nc.scalar.copy, bf01, 0, 1, 64, 128)
+        log_term(0, 3, "calc3")
+        difference(diff0[:, 2, :], 0, 2, 0, M)
+        bf11 = new_bf(1, 1, "bf0")
+        cast_w1(nc.scalar.copy, bf11, 1, 1, 0, 64)
+        cast_w1(nc.scalar.copy, bf11, 1, 1, 64, 128)
+        difference(diff0[:, 3, :], 0, 3, 0, M)
+        bf21 = new_bf(2, 1, "bf1")
+        cast_w1(nc.scalar.copy, bf21, 2, 1, 0, 64)
+        quant_w1(0, 1, bf01, 1)
+        cast_w1(nc.vector.tensor_copy, bf21, 2, 1, 64, 128)
+        quant_w1(1, 1, bf11, 1)
+        quant_w1(2, 1, bf21, 1)
+        for t in range(4):
+            for a in range(KP):
+                stage1_pass(a, 1, t)
+        mix_v = mix.rearrange("(i p) m -> p i m", p=P)
+        mix_a = keep.tile([P, 4, M], F32, name="mix_a", tag="tab1", align_bytes=64)
+        nc.sync.dma_start(out=mix_a[:], in_=mix_v[:, 0:4, :])
+        mix_b = keep.tile([P, 2, M], F32, name="mix_b", tag="raw1", align_bytes=64)
+        nc.sync.dma_start(out=mix_b[:], in_=mix_v[:, 4:6, :])
+        mix_pairs = [mix_a[:, 0:2, :], mix_a[:, 2:4, :], mix_b[:]]
+        w4_w = keep.tile([P, HP, 2 * N], U8, name="w4_w", tag="scales", align_bytes=64)
+        nc.sync.dma_start(out=w4_w[:].bitcast(I32), in_=w4_words.rearrange("a p c -> p a c").bitcast(I32))
+        w4_s = keep.tile([P, HP, N], U8, name="w4_s", tag="bf2", align_bytes=64)
+        nc.vector.memset(w4_s[:].rearrange("p a c -> p (a c)").bitcast(I32), 0)
+        for q in range(4):
+            nc.sync.dma_start(
+                out=w4_s[32 * q : 32 * q + 4, :, :].bitcast(I32),
+                in_=w4_scales[:, 4 * q : 4 * q + 4, :].rearrange("a r c -> r a c").bitcast(I32),
+            )
+        z0_bf = scale_z(diff0[:], 0, M, "0", "bf1")
+
+        HM = M // 2
+        diff1 = keep.tile([P, 6, HM], F32, name="diff1")
+        first = (2, 0)
+
+        def difference1(half, t):
+            difference(diff1[:, first[half] + t, :], 1, t, half * HM, (half + 1) * HM)
+
+        evacuate(1, 0, nc.scalar.copy)
+        evacuate(1, 1, nc.scalar.copy)
+        log_term(1, 0, "calc0")
+        z0_c, z0_s = quant_z(z0_bf, M, "0")
+        evacuate(1, 2, nc.scalar.copy)
+        log_term(1, 1, "calc1")
+        difference1(0, 0)
+        difference1(1, 0)
+        evacuate(1, 3, nc.scalar.copy)
+        log_term(1, 2, "calc2")
+        difference1(0, 1)
+        difference1(1, 1)
+        log_term(1, 3, "calc3")
+        difference1(0, 2)
+        difference1(0, 3)
+
+        out_v = out.rearrange("(i p) m -> p i m", p=P)
+        ys = {}
+
+        def stage2(half, z1_c, z1_s):
+            m0 = half * HM
+            for pair in range(N // P // 2):
+                y = psum.tile([P, 2, HM], F32, name="bank%d%d" % (pair, half))
+                ys[(half, pair)] = y
+                for i in range(2):
+                    n0 = (2 * pair + i) * P
+                    for b in range(HP):
+                        nc.tensor.matmul_mx(
+                            out=y[:, i, :],
+                            lhsT=w4_w[:, b, 2 * n0 : 2 * (n0 + P)].bitcast(FP4X4),
+                            lhsT_scale=w4_s[:, b, n0 : n0 + P],
+                            rhs=(z0_c[:, m0 : m0 + HM] if b == 0 else z1_c[:]).bitcast(FP8X4),
+                            rhs_scale=z0_s[:, m0 : m0 + HM] if b == 0 else z1_s[:],
+                            start=(b == 0),
+                            stop=(b == HP - 1),
+                        )
+
+        def finish(half, pair):
+            m0 = half * HM
+            act = ring.tile([P, 2, HM], F32, name="act")
+            nc.scalar.activation(act[:], ys[(half, pair)][:], ACT.Silu)
+            res = ring.tile([P, 2, HM], F32, name="res")
+            nc.vector.tensor_tensor(res[:], act[:], mix_pairs[pair][:, :, m0 : m0 + HM], ALU.mult)
+            nc.sync.dma_start(out=out_v[:, 2 * pair : 2 * pair + 2, m0 : m0 + HM], in_=res[:])
+
+        za_bf = scale_z(diff1[:, 2:6, :], 1, HM, "1a", "z1a")
+        difference1(1, 2)
+        stage2(0, *quant_z(za_bf, HM, "1a"))
+        difference1(1, 3)
+        zb_bf = scale_z(diff1[:, 0:4, :], 1, HM, "1b", "z1b")
+        finish(0, 0)
+        stage2(1, *quant_z(zb_bf, HM, "1b"))
+        finish(0, 1)
+        finish(0, 2)
+        for pair in range(N // P // 2):
+            finish(1, pair)

@@ -33,63 +33,78 @@ def tile_list_kiln_zone_scores_kernel(tc, tab_words, tab_scales, offs, pos1, pos
         offs_sb = keep.tile([P, S // 16], U16, name="offs_sb")
         pos1_sb = keep.tile([P, M // 16], U16, name="pos1_sb")
         pos2_sb = keep.tile([P, M // 16], U16, name="pos2_sb")
-        tab_w = [keep.tile([P, T], U16, name="tab_w%d" % a, tag="tab%d" % a, align_bytes=64) for a in range(KP)]
         tab_s = keep.tile([P, T], U8, name="tab_s", tag="scales", align_bytes=64)
-        v_w = [keep.tile([P, S], U16, name="v_w%d" % a, align_bytes=64) for a in range(KP)]
+        picked_s = keep.tile([P, S], U8, name="picked_s", align_bytes=64)
+        v_w = {}
         v_s = [keep.tile([P, S], U8, name="v_s%d" % a, align_bytes=64) for a in range(KP)]
-        gain_sb = [keep.tile([P, 4], F32, name="gain_sb%d" % b) for b in range(HP)]
+        gain_sb = keep.tile([P, HP, 4], F32, name="gain_sb")
         ngain = keep.tile([P, HP, 4], F32, name="ngain")
+        tab_w = {}
         w1_c = {}
         w1_s = {}
         w1_raw = {}
+        first_row = (0, 16, 112)
 
-        nc.vector.memset(tab_s[:].bitcast(I32), 0)
-        for a in range(1, KP):
-            nc.vector.memset(v_s[a][96:128, :].bitcast(I32), 0)
+        nc.vector.memset(tab_s[32:64, :].bitcast(I32), 0)
+        nc.vector.memset(tab_s[64:112, :].bitcast(I32), 0)
+        for a in range(KP):
+            nc.vector.memset(v_s[a][:].bitcast(I32), 0)
 
-        def load_tab(a, parts):
-            w = T // 2 // parts
-            for i in range(parts):
-                nc.sync.dma_start(out=tab_w[a][:].bitcast(I32)[:, i * w : (i + 1) * w], in_=tab_words[a].bitcast(I32)[:, i * w : (i + 1) * w])
+        def load_tab(a, tag):
+            tab_w[a] = keep.tile([P, T], U16, name="tab_w%d" % a, tag=tag, align_bytes=64)
+            nc.sync.dma_start(out=tab_w[a][:].bitcast(I32), in_=tab_words[a].bitcast(I32))
 
-        def load_w1(a, b, tag):
-            raw = keep.tile([P, 2, 4, 256], F32, name="w1_raw%d%d" % (a, b), tag=tag, align_bytes=64)
-            for u in range(2):
-                rows = w1[512 * a : 512 * (a + 1), 512 * b + 256 * u : 512 * b + 256 * (u + 1)]
-                nc.sync.dma_start(out=raw[:, u], in_=rows.rearrange("(p j) c -> p j c", j=4))
-            w1_raw[(a, b)] = raw
+        def new_raw(a, b, tag, parts):
+            w1_raw[(a, b)] = keep.tile([P, parts, 4, 512 // parts], F32, name="w1_raw%d%d" % (a, b), tag=tag, align_bytes=64)
 
-        gain_v = gain.rearrange("(b p t) -> b p t", b=HP, t=4)
-        nc.sync.dma_start(offs_sb[:], offs)
-        nc.sync.dma_start(pos1_sb[:], pos1)
-        nc.sync.dma_start(pos2_sb[:], pos2)
-        nc.sync.dma_start(out=gain_sb[0][:], in_=gain_v[0])
-        load_tab(0, 2)
-        load_w1(0, 0, "raw0")
-        nc.sync.dma_start(out=gain_sb[1][:], in_=gain_v[1])
-        for q in range(4):
-            (nc.scalar if q < 2 else nc.sync).dma_start(
-                out=tab_s[32 * q : 32 * q + 4 * KP, :].bitcast(I32),
-                in_=tab_scales[:, 4 * q : 4 * q + 4, :].bitcast(I32),
-            )
-        load_tab(1, 1)
-        load_w1(1, 0, "raw1")
-        load_tab(2, 1)
+        def load_w1(a, b, u):
+            raw = w1_raw[(a, b)]
+            w = raw.shape[3]
+            rows = w1[512 * a : 512 * (a + 1), 512 * b + w * u : 512 * b + w * (u + 1)]
+            nc.sync.dma_start(out=raw[:, u], in_=rows.rearrange("(p j) c -> p j c", j=4))
 
-        def gather_words(a):
+        def load_w1_whole(a, b, tag):
+            new_raw(a, b, tag, 1)
+            load_w1(a, b, 0)
+
+        def gather_words(a, tag):
+            v_w[a] = keep.tile([P, S], U16, name="v_w%d" % a, tag=tag, align_bytes=64)
             nc.vector.tensor_copy(v_w[a][:], tab_w[a][:].indirect(offs_sb[:]))
 
-        def gather_scales():
-            nc.vector.tensor_copy(v_s[0][:], tab_s[:].indirect(offs_sb[:]))
-            for a in range(1, KP):
-                nc.sync.dma_start(
-                    out=v_s[a][0:100, :].bitcast(I32),
-                    in_=v_s[0][4 * a : 4 * a + 100, :].bitcast(I32),
-                )
+        def move_plane(a, q):
+            r0 = first_row[a] + 4 * q
+            nc.sync.dma_start(out=v_s[a][32 * q : 32 * q + 4, :].bitcast(I32), in_=picked_s[r0 : r0 + 4, :].bitcast(I32))
+
+        scale_rows = tab_scales.rearrange("a q t -> (a q) t").bitcast(I32)
+        nc.sync.dma_start(offs_sb[:], offs)
+        nc.sync.dma_start(out=tab_s[0:32, :].bitcast(I32), in_=scale_rows[0:32, :])
+        nc.sync.dma_start(out=tab_s[112:128, :].bitcast(I32), in_=scale_rows[32:48, :])
+        nc.sync.dma_start(pos1_sb[:], pos1)
+        nc.sync.dma_start(pos2_sb[:], pos2)
+        nc.sync.dma_start(out=gain_sb[:], in_=gain.rearrange("(b p t) -> p b t", b=HP, t=4))
+        load_tab(0, "tab0")
+        load_w1_whole(0, 0, "raw0")
+        load_tab(1, "tab1")
+        nc.vector.tensor_copy(picked_s[:], tab_s[:].indirect(offs_sb[:]))
+        gather_words(0, "vw0")
+        for q in range(4):
+            move_plane(0, q)
+        new_raw(1, 0, "scales", 2)
+        load_w1(1, 0, 0)
+        load_w1(1, 0, 1)
+        move_plane(1, 0)
+        move_plane(1, 1)
+        load_tab(2, "tab0")
+        move_plane(1, 2)
+        move_plane(1, 3)
+        move_plane(2, 0)
+        move_plane(2, 1)
 
         def cast_w1(copy, w_bf, a, b, m0, m1):
-            u = m0 // 64
-            src = w1_raw[(a, b)][:, u].rearrange("p j (m t) -> p m j t", t=4)[:, m0 - 64 * u : m1 - 64 * u]
+            raw = w1_raw[(a, b)]
+            per = raw.shape[3] // 4
+            u = m0 // per
+            src = raw[:, u].rearrange("p j (m t) -> p m j t", t=4)[:, m0 - per * u : m1 - per * u]
             dst = w_bf[:].rearrange("p t m j -> p m j t")[:, m0:m1]
             copy(dst, src)
 
@@ -125,21 +140,23 @@ def tile_list_kiln_zone_scores_kernel(tc, tab_words, tab_scales, offs, pos1, pos
                     stop=(a == KP - 1),
                 )
 
-        gather_words(0)
-        gather_scales()
-        load_w1(2, 0, "scales")
         w_bf = new_bf(0, 0, "bf0")
         cast_w1(nc.scalar.copy, w_bf, 0, 0, 0, 64)
         cast_w1(nc.scalar.copy, w_bf, 0, 0, 64, 128)
+        new_raw(2, 0, "raw0", 2)
+        load_w1(2, 0, 0)
+        load_w1(2, 0, 1)
+        move_plane(2, 2)
+        move_plane(2, 3)
         quant_w1(0, 0, w_bf, 1)
         for t in range(4):
             stage1_pass(0, 0, t)
-        gather_words(1)
+        gather_words(1, "bf0")
         w_bf = new_bf(1, 0, "bf1")
         cast_w1(nc.scalar.copy, w_bf, 1, 0, 0, 64)
         cast_w1(nc.scalar.copy, w_bf, 1, 0, 64, 128)
         quant_w1(1, 0, w_bf, 1)
-        gather_words(2)
+        gather_words(2, "vw2")
         w_bf = new_bf(2, 0, "bf2")
         cast_w1(nc.scalar.copy, w_bf, 2, 0, 0, 64)
         cast_w1(nc.vector.tensor_copy, w_bf, 2, 0, 64, 64 + SPLIT)
@@ -148,11 +165,10 @@ def tile_list_kiln_zone_scores_kernel(tc, tab_words, tab_scales, offs, pos1, pos
         for t in range(4):
             stage1_pass(1, 0, t)
             stage1_pass(2, 0, t)
-        load_w1(0, 1, "tab1")
-        load_w1(1, 1, "raw1")
-        load_w1(2, 1, "tab2")
-        for b in range(HP):
-            nc.vector.tensor_scalar(ngain[:, b, :], gain_sb[b][:], -1.0, None, ALU.mult)
+        load_w1_whole(0, 1, "tab1")
+        load_w1_whole(1, 1, "scales")
+        load_w1_whole(2, 1, "tab0")
+        nc.vector.tensor_scalar(ngain[:], gain_sb[:], -1.0, None, ALU.mult)
 
         h = {}
         logs = {}
@@ -177,9 +193,9 @@ def tile_list_kiln_zone_scores_kernel(tc, tab_words, tab_scales, offs, pos1, pos
         def scale_z(diff, b, width, name, tag):
             z_bf = keep.tile([P, width, 4], BF16, name="z_bf" + name, tag=tag, align_bytes=64)
             nc.vector.tensor_tensor(
-                z_bf[:].rearrange("p (c i) t -> p c t i", i=4),
-                diff.rearrange("p t (c i) -> p c t i", i=4),
-                ngain[:, b, :].unsqueeze(1).unsqueeze(3).to_broadcast([P, width // 4, 4, 4]),
+                z_bf[:].rearrange("p (c i) t -> p c t i", i=2),
+                diff.rearrange("p t (c i) -> p c t i", i=2),
+                ngain[:, b, :].unsqueeze(1).unsqueeze(3).to_broadcast([P, width // 2, 4, 2]),
                 ALU.mult,
             )
             return z_bf
@@ -205,7 +221,7 @@ def tile_list_kiln_zone_scores_kernel(tc, tab_words, tab_scales, offs, pos1, pos
         cast_w1(nc.scalar.copy, bf01, 0, 1, 64, 128)
         log_term(0, 3, "calc3")
         difference(diff0[:, 2, :], 0, 2, 0, M)
-        bf11 = new_bf(1, 1, "bf0")
+        bf11 = new_bf(1, 1, "bf3")
         cast_w1(nc.scalar.copy, bf11, 1, 1, 0, 64)
         cast_w1(nc.scalar.copy, bf11, 1, 1, 64, 128)
         difference(diff0[:, 3, :], 0, 3, 0, M)
@@ -221,19 +237,29 @@ def tile_list_kiln_zone_scores_kernel(tc, tab_words, tab_scales, offs, pos1, pos
         mix_v = mix.rearrange("(i p) m -> p i m", p=P)
         mix_a = keep.tile([P, 4, M], F32, name="mix_a", tag="tab1", align_bytes=64)
         nc.sync.dma_start(out=mix_a[:], in_=mix_v[:, 0:4, :])
-        mix_b = keep.tile([P, 2, M], F32, name="mix_b", tag="raw1", align_bytes=64)
+        mix_b = keep.tile([P, 2, M], F32, name="mix_b", tag="scales", align_bytes=64)
         nc.sync.dma_start(out=mix_b[:], in_=mix_v[:, 4:6, :])
         mix_pairs = [mix_a[:, 0:2, :], mix_a[:, 2:4, :], mix_b[:]]
-        w4_w = keep.tile([P, HP, 2 * N], U8, name="w4_w", tag="scales", align_bytes=64)
+        w4_w = keep.tile([P, HP, 2 * N], U8, name="w4_w", tag="raw0", align_bytes=64)
         nc.sync.dma_start(out=w4_w[:].bitcast(I32), in_=w4_words.rearrange("a p c -> p a c").bitcast(I32))
         w4_s = keep.tile([P, HP, N], U8, name="w4_s", tag="bf2", align_bytes=64)
-        nc.vector.memset(w4_s[:].rearrange("p a c -> p (a c)").bitcast(I32), 0)
+        nc.gpsimd.memset(w4_s[:].rearrange("p a c -> p (a c)").bitcast(I32), 0)
         for q in range(4):
             nc.sync.dma_start(
                 out=w4_s[32 * q : 32 * q + 4, :, :].bitcast(I32),
                 in_=w4_scales[:, 4 * q : 4 * q + 4, :].rearrange("a r c -> r a c").bitcast(I32),
             )
-        z0_bf = scale_z(diff0[:], 0, M, "0", "bf1")
+        z0_rows = keep.tile([P, 4, M], BF16, name="z0_rows", align_bytes=64)
+        z0_bf = keep.tile([P, M, 4], BF16, name="z0_bf", align_bytes=64)
+
+        def scale_row(t):
+            nc.scalar.activation(z0_rows[:, t, :], diff0[:, t, :], ACT.Copy, scale=ngain[:, 0, t : t + 1])
+
+        def weave(m0, m1):
+            nc.scalar.copy(
+                z0_bf[:, m0:m1, :].rearrange("p (c i) t -> p c t i", i=4),
+                z0_rows[:, :, m0:m1].rearrange("p t (c i) -> p c t i", i=4),
+            )
 
         HM = M // 2
         diff1 = keep.tile([P, 6, HM], F32, name="diff1")
@@ -244,17 +270,23 @@ def tile_list_kiln_zone_scores_kernel(tc, tab_words, tab_scales, offs, pos1, pos
 
         evacuate(1, 0, nc.scalar.copy)
         evacuate(1, 1, nc.scalar.copy)
+        scale_row(0)
         log_term(1, 0, "calc0")
-        z0_c, z0_s = quant_z(z0_bf, M, "0")
         evacuate(1, 2, nc.scalar.copy)
+        scale_row(1)
         log_term(1, 1, "calc1")
         difference1(0, 0)
         difference1(1, 0)
         evacuate(1, 3, nc.scalar.copy)
+        scale_row(2)
         log_term(1, 2, "calc2")
         difference1(0, 1)
         difference1(1, 1)
+        scale_row(3)
+        weave(0, 128)
         log_term(1, 3, "calc3")
+        for m0 in range(128, M, 128):
+            weave(m0, m0 + 128)
         difference1(0, 2)
         difference1(0, 3)
 
@@ -288,6 +320,7 @@ def tile_list_kiln_zone_scores_kernel(tc, tab_words, tab_scales, offs, pos1, pos
             nc.sync.dma_start(out=out_v[:, 2 * pair : 2 * pair + 2, m0 : m0 + HM], in_=res[:])
 
         za_bf = scale_z(diff1[:, 2:6, :], 1, HM, "1a", "z1a")
+        z0_c, z0_s = quant_z(z0_bf, M, "0")
         difference1(1, 2)
         stage2(0, *quant_z(za_bf, HM, "1a"))
         difference1(1, 3)

@@ -20,7 +20,10 @@ P = 128
 KP = K // 512
 HP = H // 512
 BANK = 512
+HM = M // 2
 SPLIT = 44
+WHOLE = ((0, 512),)
+FIRST_APART = ((0, 128), (128, 512))
 
 
 def tile_list_kiln_zone_scores_kernel(tc, tab_words, tab_scales, offs, pos1, pos2, w1, gain, w4_words, w4_scales, mix, out):
@@ -112,12 +115,11 @@ def tile_list_kiln_zone_scores_kernel(tc, tab_words, tab_scales, offs, pos1, pos
             w1_c[(a, b)] = keep.tile([P, 512], U32, name="w1_c%d%d" % (a, b), align_bytes=64)
             w1_s[(a, b)] = keep.tile([P, 512], U8, name="w1_s%d%d" % (a, b), align_bytes=64)
             flat = w_bf[:].rearrange("p t m j -> p (t m j)")
-            w = 512 // parts
-            for i in range(parts):
+            for c0, c1 in parts:
                 nc.vector.quantize_mx(
-                    out=w1_c[(a, b)][:, i * w : (i + 1) * w].bitcast(FP8X4),
-                    scales=w1_s[(a, b)][:, i * w : (i + 1) * w],
-                    in_=flat[:, 4 * i * w : 4 * (i + 1) * w],
+                    out=w1_c[(a, b)][:, c0:c1].bitcast(FP8X4),
+                    scales=w1_s[(a, b)][:, c0:c1],
+                    in_=flat[:, 4 * c0 : 4 * c1],
                 )
 
         def new_bf(a, b, tag):
@@ -148,20 +150,20 @@ def tile_list_kiln_zone_scores_kernel(tc, tab_words, tab_scales, offs, pos1, pos
         load_w1(2, 0, 1)
         move_plane(2, 2)
         move_plane(2, 3)
-        quant_w1(0, 0, w_bf, 1)
+        quant_w1(0, 0, w_bf, WHOLE)
         for t in range(4):
             stage1_pass(0, 0, t)
         gather_words(1, "bf0")
         w_bf = new_bf(1, 0, "bf1")
         cast_w1(nc.scalar.copy, w_bf, 1, 0, 0, 64)
         cast_w1(nc.scalar.copy, w_bf, 1, 0, 64, 128)
-        quant_w1(1, 0, w_bf, 1)
+        quant_w1(1, 0, w_bf, WHOLE)
         gather_words(2, "vw2")
         w_bf = new_bf(2, 0, "bf2")
         cast_w1(nc.scalar.copy, w_bf, 2, 0, 0, 64)
         cast_w1(nc.vector.tensor_copy, w_bf, 2, 0, 64, 64 + SPLIT)
         cast_w1(nc.scalar.copy, w_bf, 2, 0, 64 + SPLIT, 128)
-        quant_w1(2, 0, w_bf, 4)
+        quant_w1(2, 0, w_bf, FIRST_APART)
         for t in range(4):
             stage1_pass(1, 0, t)
             stage1_pass(2, 0, t)
@@ -174,16 +176,18 @@ def tile_list_kiln_zone_scores_kernel(tc, tab_words, tab_scales, offs, pos1, pos
         logs = {}
 
         def evacuate(b, t, first_copy):
-            h[(b, t)] = keep.tile([P, S], F32, name="h%d%d" % (b, t))
+            h[(b, t)] = keep.tile([P, S], F32, name="h%d%d" % (b, t), align_bytes=64)
             first_copy(h[(b, t)][:, 0:BANK], banks[(t, 0)][:])
             nc.scalar.copy(h[(b, t)][:, BANK:S], banks[(t, 1)][:])
 
         def log_term(b, t, tag):
             calc = keep.tile([P, M], F32, name="calc%d%d" % (b, t), tag=tag, align_bytes=64)
             nc.vector.tensor_copy(calc[:], h[(b, t)][:].indirect(pos1_sb[:]))
-            logs[(b, t)] = keep.tile([P, M], F32, name="log%d%d" % (b, t))
-            nc.scalar.activation(logs[(b, t)][:], calc[:], ACT.Square)
-            nc.scalar.activation(logs[(b, t)][:], logs[(b, t)][:], ACT.Ln, bias=1.0)
+            logs[(b, t)] = keep.tile([P, M], F32, name="log%d%d" % (b, t), align_bytes=64)
+            for m0 in (0, HM):
+                nc.scalar.activation(logs[(b, t)][:, m0 : m0 + HM], calc[:, m0 : m0 + HM], ACT.Square)
+            for m0 in (0, HM):
+                nc.scalar.activation(logs[(b, t)][:, m0 : m0 + HM], logs[(b, t)][:, m0 : m0 + HM], ACT.Ln, bias=1.0)
 
         def difference(dst, b, t, m0, m1):
             nc.vector.tensor_tensor(
@@ -209,28 +213,28 @@ def tile_list_kiln_zone_scores_kernel(tc, tab_words, tab_scales, offs, pos1, pos
         diff0 = keep.tile([P, 4, M], F32, name="diff0")
         evacuate(0, 0, nc.vector.tensor_copy)
         evacuate(0, 1, nc.scalar.copy)
-        log_term(0, 0, "late")
         evacuate(0, 2, nc.scalar.copy)
+        log_term(0, 0, "late")
+        evacuate(0, 3, nc.scalar.copy)
         log_term(0, 1, "calc1")
         difference(diff0[:, 0, :], 0, 0, 0, M)
-        evacuate(0, 3, nc.scalar.copy)
         bf01 = new_bf(0, 1, "late")
         cast_w1(nc.scalar.copy, bf01, 0, 1, 0, 64)
+        cast_w1(nc.scalar.copy, bf01, 0, 1, 64, 128)
         log_term(0, 2, "calc2")
         difference(diff0[:, 1, :], 0, 1, 0, M)
-        cast_w1(nc.scalar.copy, bf01, 0, 1, 64, 128)
+        bf11 = new_bf(1, 1, "log01")
+        bf21 = new_bf(2, 1, "h01")
+        cast_w1(nc.scalar.copy, bf11, 1, 1, 0, 64)
+        cast_w1(nc.scalar.copy, bf21, 2, 1, 0, 64)
+        quant_w1(0, 1, bf01, WHOLE)
+        cast_w1(nc.vector.tensor_copy, bf11, 1, 1, 64, 128)
+        cast_w1(nc.vector.tensor_copy, bf21, 2, 1, 64, 128)
         log_term(0, 3, "calc3")
         difference(diff0[:, 2, :], 0, 2, 0, M)
-        bf11 = new_bf(1, 1, "bf3")
-        cast_w1(nc.scalar.copy, bf11, 1, 1, 0, 64)
-        cast_w1(nc.scalar.copy, bf11, 1, 1, 64, 128)
+        quant_w1(1, 1, bf11, WHOLE)
+        quant_w1(2, 1, bf21, FIRST_APART)
         difference(diff0[:, 3, :], 0, 3, 0, M)
-        bf21 = new_bf(2, 1, "bf1")
-        cast_w1(nc.scalar.copy, bf21, 2, 1, 0, 64)
-        quant_w1(0, 1, bf01, 1)
-        cast_w1(nc.vector.tensor_copy, bf21, 2, 1, 64, 128)
-        quant_w1(1, 1, bf11, 1)
-        quant_w1(2, 1, bf21, 1)
         for t in range(4):
             for a in range(KP):
                 stage1_pass(a, 1, t)
@@ -249,19 +253,10 @@ def tile_list_kiln_zone_scores_kernel(tc, tab_words, tab_scales, offs, pos1, pos
                 out=w4_s[32 * q : 32 * q + 4, :, :].bitcast(I32),
                 in_=w4_scales[:, 4 * q : 4 * q + 4, :].rearrange("a r c -> r a c").bitcast(I32),
             )
-        z0_rows = keep.tile([P, 4, M], BF16, name="z0_rows", align_bytes=64)
-        z0_bf = keep.tile([P, M, 4], BF16, name="z0_bf", align_bytes=64)
+        z0a_bf = scale_z(diff0[:, :, 0:HM], 0, HM, "0a", "h01")
+        z0b_rows = keep.tile([P, 4, HM], BF16, name="z0b_rows", align_bytes=64)
+        z0b_bf = keep.tile([P, HM, 4], BF16, name="z0b_bf", align_bytes=64)
 
-        def scale_row(t):
-            nc.scalar.activation(z0_rows[:, t, :], diff0[:, t, :], ACT.Copy, scale=ngain[:, 0, t : t + 1])
-
-        def weave(m0, m1):
-            nc.scalar.copy(
-                z0_bf[:, m0:m1, :].rearrange("p (c i) t -> p c t i", i=4),
-                z0_rows[:, :, m0:m1].rearrange("p t (c i) -> p c t i", i=4),
-            )
-
-        HM = M // 2
         diff1 = keep.tile([P, 6, HM], F32, name="diff1")
         first = (2, 0)
 
@@ -270,31 +265,31 @@ def tile_list_kiln_zone_scores_kernel(tc, tab_words, tab_scales, offs, pos1, pos
 
         evacuate(1, 0, nc.scalar.copy)
         evacuate(1, 1, nc.scalar.copy)
-        scale_row(0)
-        log_term(1, 0, "calc0")
         evacuate(1, 2, nc.scalar.copy)
-        scale_row(1)
+        log_term(1, 0, "calc0")
+        z0a = quant_z(z0a_bf, HM, "0a")
+        evacuate(1, 3, nc.scalar.copy)
         log_term(1, 1, "calc1")
         difference1(0, 0)
         difference1(1, 0)
-        evacuate(1, 3, nc.scalar.copy)
-        scale_row(2)
         log_term(1, 2, "calc2")
         difference1(0, 1)
         difference1(1, 1)
-        scale_row(3)
-        weave(0, 128)
         log_term(1, 3, "calc3")
-        for m0 in range(128, M, 128):
-            weave(m0, m0 + 128)
+        for t in range(4):
+            nc.scalar.activation(z0b_rows[:, t, :], diff0[:, t, HM:M], ACT.Copy, scale=ngain[:, 0, t : t + 1])
+        for m0 in (0, HM // 2):
+            nc.scalar.copy(
+                z0b_bf[:, m0 : m0 + HM // 2, :].rearrange("p (c i) t -> p c t i", i=4),
+                z0b_rows[:, :, m0 : m0 + HM // 2].rearrange("p t (c i) -> p c t i", i=4),
+            )
         difference1(0, 2)
         difference1(0, 3)
 
         out_v = out.rearrange("(i p) m -> p i m", p=P)
         ys = {}
 
-        def stage2(half, z1_c, z1_s):
-            m0 = half * HM
+        def stage2(half, z):
             for pair in range(N // P // 2):
                 y = psum.tile([P, 2, HM], F32, name="bank%d%d" % (pair, half))
                 ys[(half, pair)] = y
@@ -305,8 +300,8 @@ def tile_list_kiln_zone_scores_kernel(tc, tab_words, tab_scales, offs, pos1, pos
                             out=y[:, i, :],
                             lhsT=w4_w[:, b, 2 * n0 : 2 * (n0 + P)].bitcast(FP4X4),
                             lhsT_scale=w4_s[:, b, n0 : n0 + P],
-                            rhs=(z0_c[:, m0 : m0 + HM] if b == 0 else z1_c[:]).bitcast(FP8X4),
-                            rhs_scale=z0_s[:, m0 : m0 + HM] if b == 0 else z1_s[:],
+                            rhs=z[b][0][:].bitcast(FP8X4),
+                            rhs_scale=z[b][1][:],
                             start=(b == 0),
                             stop=(b == HP - 1),
                         )
@@ -315,18 +310,18 @@ def tile_list_kiln_zone_scores_kernel(tc, tab_words, tab_scales, offs, pos1, pos
             m0 = half * HM
             act = ring.tile([P, 2, HM], F32, name="act")
             nc.scalar.activation(act[:], ys[(half, pair)][:], ACT.Silu)
-            res = ring.tile([P, 2, HM], F32, name="res")
+            res = keep.tile([P, 2, HM], F32, name="res%d%d" % (half, pair))
             nc.vector.tensor_tensor(res[:], act[:], mix_pairs[pair][:, :, m0 : m0 + HM], ALU.mult)
             nc.sync.dma_start(out=out_v[:, 2 * pair : 2 * pair + 2, m0 : m0 + HM], in_=res[:])
 
         za_bf = scale_z(diff1[:, 2:6, :], 1, HM, "1a", "z1a")
-        z0_c, z0_s = quant_z(z0_bf, M, "0")
         difference1(1, 2)
-        stage2(0, *quant_z(za_bf, HM, "1a"))
+        stage2(0, (z0a, quant_z(za_bf, HM, "1a")))
         difference1(1, 3)
         zb_bf = scale_z(diff1[:, 0:4, :], 1, HM, "1b", "z1b")
+        z0b = quant_z(z0b_bf, HM, "0b")
         finish(0, 0)
-        stage2(1, *quant_z(zb_bf, HM, "1b"))
+        stage2(1, (z0b, quant_z(zb_bf, HM, "1b")))
         finish(0, 1)
         finish(0, 2)
         for pair in range(N // P // 2):

@@ -53,6 +53,10 @@ def tile_list_kiln_zone_scores_kernel(tc, tab_words, tab_scales, offs, pos1, pos
         for a in range(KP):
             nc.vector.memset(v_s[a][:].bitcast(I32), 0)
 
+        warm = keep.tile([P, 2], F32, name="warm")
+        nc.vector.memset(warm[:, 0:1], 1.0)
+        nc.scalar.activation(warm[:, 1:2], warm[:, 0:1], ACT.Ln, bias=1.0)
+
         def load_tab(a, tag):
             tab_w[a] = keep.tile([P, T], U16, name="tab_w%d" % a, tag=tag, align_bytes=64)
             nc.sync.dma_start(out=tab_w[a][:].bitcast(I32), in_=tab_words[a].bitcast(I32))

from contextlib import ExitStack

import concourse.mybir as mybir

K, H, N, T, S, M = 1536, 1024, 768, 4096, 1024, 512
FLOPS = 2 * K * H * S + 2 * H * N * M

F32 = mybir.dt.float32
BF16 = mybir.dt.bfloat16
I32 = mybir.dt.int32
U32 = mybir.dt.uint32
U16 = mybir.dt.uint16
U8 = mybir.dt.uint8
FP8X4 = mybir.dt.float8_e4m3fn_x4
FP4X4 = mybir.dt.float4_e2m1fn_x4
ACT = mybir.ActivationFunctionType
ALU = mybir.AluOpType

P = 128
KP = K // 512
HP = H // 512
BANK = 512
HM = M // 2
SPLIT = 44
WHOLE = ((0, 512),)
FIRST_APART = ((0, 128), (128, 512))


def tile_list_kiln_zone_scores_kernel(tc, tab_words, tab_scales, offs, pos1, pos2, w1, gain, w4_words, w4_scales, mix, out):
    nc = tc.nc
    with ExitStack() as ctx:
        keep = ctx.enter_context(tc.tile_pool(name="keep", bufs=1))
        ring = ctx.enter_context(tc.tile_pool(name="ring", bufs=3))
        psum = ctx.enter_context(tc.psum_pool(name="psum", bufs=1))

        offs_sb = keep.tile([P, S // 16], U16, name="offs_sb")
        pos1_sb = keep.tile([P, M // 16], U16, name="pos1_sb")
        pos2_sb = keep.tile([P, M // 16], U16, name="pos2_sb")
        tab_s = keep.tile([P, T], U8, name="tab_s", tag="scales", align_bytes=64)
        picked_s = keep.tile([P, S], U8, name="picked_s", align_bytes=64)
        v_w = {}
        v_s = [keep.tile([P, S], U8, name="v_s%d" % a, align_bytes=64) for a in range(KP)]
        gain_sb = keep.tile([P, HP, 4], F32, name="gain_sb")
        ngain = keep.tile([P, HP, 4], F32, name="ngain")
        tab_w = {}
        w1_c = {}
        w1_s = {}
        w1_raw = {}
        first_row = (0, 16, 112)

        nc.vector.memset(tab_s[32:64, :].bitcast(I32), 0)
        nc.vector.memset(tab_s[64:112, :].bitcast(I32), 0)
        for a in range(KP):
            nc.vector.memset(v_s[a][:].bitcast(I32), 0)

        warm = keep.tile([P, 2], F32, name="warm")
        nc.vector.memset(warm[:, 0:1], 1.0)
        nc.scalar.activation(warm[:, 1:2], warm[:, 0:1], ACT.Ln, bias=1.0)

        def load_tab(a, tag):
            tab_w[a] = keep.tile([P, T], U16, name="tab_w%d" % a, tag=tag, align_bytes=64)
            nc.sync.dma_start(out=tab_w[a][:].bitcast(I32), in_=tab_words[a].bitcast(I32))

        def new_raw(a, b, tag, parts):
            w1_raw[(a, b)] = keep.tile([P, parts, 4, 512 // parts], F32, name="w1_raw%d%d" % (a, b), tag=tag, align_bytes=64)

        def load_w1(a, b, u):
            raw = w1_raw[(a, b)]
            w = raw.shape[3]
            rows = w1[512 * a : 512 * (a + 1), 512 * b + w * u : 512 * b + w * (u + 1)]
            nc.sync.dma_start(out=raw[:, u], in_=rows.rearrange("(p j) c -> p j c", j=4))

        def load_w1_whole(a, b, tag):
            new_raw(a, b, tag, 1)
            load_w1(a, b, 0)

        def gather_words(a, tag):
            v_w[a] = keep.tile([P, S], U16, name="v_w%d" % a, tag=tag, align_bytes=64)
            nc.vector.tensor_copy(v_w[a][:], tab_w[a][:].indirect(offs_sb[:]))

        def move_plane(a, q):
            r0 = first_row[a] + 4 * q
            nc.sync.dma_start(out=v_s[a][32 * q : 32 * q + 4, :].bitcast(I32), in_=picked_s[r0 : r0 + 4, :].bitcast(I32))

        scale_rows = tab_scales.rearrange("a q t -> (a q) t").bitcast(I32)
        nc.sync.dma_start(offs_sb[:], offs)
        nc.sync.dma_start(out=tab_s[0:32, :].bitcast(I32), in_=scale_rows[0:32, :])
        nc.sync.dma_start(out=tab_s[112:128, :].bitcast(I32), in_=scale_rows[32:48, :])
        nc.sync.dma_start(pos1_sb[:], pos1)
        nc.sync.dma_start(pos2_sb[:], pos2)
        nc.sync.dma_start(out=gain_sb[:], in_=gain.rearrange("(b p t) -> p b t", b=HP, t=4))
        load_tab(0, "tab0")
        load_w1_whole(0, 0, "raw0")
        load_tab(1, "tab1")
        nc.vector.tensor_copy(picked_s[:], tab_s[:].indirect(offs_sb[:]))
        gather_words(0, "vw0")
        for q in range(4):
            move_plane(0, q)
        new_raw(1, 0, "scales", 2)
        load_w1(1, 0, 0)
        load_w1(1, 0, 1)
        move_plane(1, 0)
        move_plane(1, 1)
        load_tab(2, "tab0")
        move_plane(1, 2)
        move_plane(1, 3)
        move_plane(2, 0)
        move_plane(2, 1)

        def cast_w1(copy, w_bf, a, b, m0, m1):
            raw = w1_raw[(a, b)]
            per = raw.shape[3] // 4
            u = m0 // per
            src = raw[:, u].rearrange("p j (m t) -> p m j t", t=4)[:, m0 - per * u : m1 - per * u]
            dst = w_bf[:].rearrange("p t m j -> p m j t")[:, m0:m1]
            copy(dst, src)

        def quant_w1(a, b, w_bf, parts):
            w1_c[(a, b)] = keep.tile([P, 512], U32, name="w1_c%d%d" % (a, b), align_bytes=64)
            w1_s[(a, b)] = keep.tile([P, 512], U8, name="w1_s%d%d" % (a, b), align_bytes=64)
            flat = w_bf[:].rearrange("p t m j -> p (t m j)")
            for c0, c1 in parts:
                nc.vector.quantize_mx(
                    out=w1_c[(a, b)][:, c0:c1].bitcast(FP8X4),
                    scales=w1_s[(a, b)][:, c0:c1],
                    in_=flat[:, 4 * c0 : 4 * c1],
                )

        def new_bf(a, b, tag):
            return keep.tile([P, 4, P, 4], BF16, name="w_bf%d%d" % (a, b), tag=tag, align_bytes=64)

        banks = {}

        def stage1_pass(a, b, t):
            for half in range(2):
                if a == 0:
                    banks[(t, half)] = psum.tile([P, BANK], F32, name="bank%d%d" % (t, half))
                cols = slice(half * BANK, (half + 1) * BANK)
                nc.tensor.matmul_mx(
                    out=banks[(t, half)][:],
                    lhsT=w1_c[(a, b)][:, t * P : (t + 1) * P].bitcast(FP8X4),
                    lhsT_scale=w1_s[(a, b)][:, t * P : (t + 1) * P],
                    rhs=v_w[a][:, cols].bitcast(FP4X4),
                    rhs_scale=v_s[a][:, cols],
                    start=(a == 0),
                    stop=(a == KP - 1),
                )

        w_bf = new_bf(0, 0, "bf0")
        cast_w1(nc.scalar.copy, w_bf, 0, 0, 0, 64)
        cast_w1(nc.scalar.copy, w_bf, 0, 0, 64, 128)
        new_raw(2, 0, "raw0", 2)
        load_w1(2, 0, 0)
        load_w1(2, 0, 1)
        move_plane(2, 2)
        move_plane(2, 3)
        quant_w1(0, 0, w_bf, WHOLE)
        for t in range(4):
            stage1_pass(0, 0, t)
        gather_words(1, "bf0")
        w_bf = new_bf(1, 0, "bf1")
        cast_w1(nc.scalar.copy, w_bf, 1, 0, 0, 64)
        cast_w1(nc.scalar.copy, w_bf, 1, 0, 64, 128)
        quant_w1(1, 0, w_bf, WHOLE)
        gather_words(2, "vw2")
        w_bf = new_bf(2, 0, "bf2")
        cast_w1(nc.scalar.copy, w_bf, 2, 0, 0, 64)
        cast_w1(nc.vector.tensor_copy, w_bf, 2, 0, 64, 64 + SPLIT)
        cast_w1(nc.scalar.copy, w_bf, 2, 0, 64 + SPLIT, 128)
        quant_w1(2, 0, w_bf, FIRST_APART)
        for t in range(4):
            stage1_pass(1, 0, t)
            stage1_pass(2, 0, t)
        load_w1_whole(0, 1, "tab1")
        load_w1_whole(1, 1, "scales")
        load_w1_whole(2, 1, "tab0")
        nc.vector.tensor_scalar(ngain[:], gain_sb[:], -1.0, None, ALU.mult)

        h = {}
        logs = {}

        def evacuate(b, t, first_copy):
            h[(b, t)] = keep.tile([P, S], F32, name="h%d%d" % (b, t), align_bytes=64)
            first_copy(h[(b, t)][:, 0:BANK], banks[(t, 0)][:])
            nc.scalar.copy(h[(b, t)][:, BANK:S], banks[(t, 1)][:])

        def log_term(b, t, tag):
            calc = keep.tile([P, M], F32, name="calc%d%d" % (b, t), tag=tag, align_bytes=64)
            nc.vector.tensor_copy(calc[:], h[(b, t)][:].indirect(pos1_sb[:]))
            logs[(b, t)] = keep.tile([P, M], F32, name="log%d%d" % (b, t), align_bytes=64)
            for m0 in (0, HM):
                nc.scalar.activation(logs[(b, t)][:, m0 : m0 + HM], calc[:, m0 : m0 + HM], ACT.Square)
            for m0 in (0, HM):
                nc.scalar.activation(logs[(b, t)][:, m0 : m0 + HM], logs[(b, t)][:, m0 : m0 + HM], ACT.Ln, bias=1.0)

        def difference(dst, b, t, m0, m1):
            nc.vector.tensor_tensor(
                dst, h[(b, t)][:].indirect(pos2_sb[:, m0 // 16 : m1 // 16]), logs[(b, t)][:, m0:m1], ALU.subtract
            )

        def scale_z(diff, b, width, name, tag):
            z_bf = keep.tile([P, width, 4], BF16, name="z_bf" + name, tag=tag, align_bytes=64)
            nc.vector.tensor_tensor(
                z_bf[:].rearrange("p (c i) t -> p c t i", i=2),
                diff.rearrange("p t (c i) -> p c t i", i=2),
                ngain[:, b, :].unsqueeze(1).unsqueeze(3).to_broadcast([P, width // 2, 4, 2]),
                ALU.mult,
            )
            return z_bf

        def quant_z(z_bf, width, name):
            z_c = keep.tile([P, width], U32, name="z_c" + name, align_bytes=64)
            z_s = keep.tile([P, width], U8, name="z_s" + name, align_bytes=64)
            nc.vector.quantize_mx(out=z_c[:].bitcast(FP8X4), scales=z_s[:], in_=z_bf[:].rearrange("p m t -> p (m t)"))
            return z_c, z_s

        diff0 = keep.tile([P, 4, M], F32, name="diff0")
        evacuate(0, 0, nc.vector.tensor_copy)
        evacuate(0, 1, nc.scalar.copy)
        evacuate(0, 2, nc.scalar.copy)
        log_term(0, 0, "late")
        evacuate(0, 3, nc.scalar.copy)
        log_term(0, 1, "calc1")
        difference(diff0[:, 0, :], 0, 0, 0, M)
        bf01 = new_bf(0, 1, "late")
        cast_w1(nc.scalar.copy, bf01, 0, 1, 0, 64)
        cast_w1(nc.scalar.copy, bf01, 0, 1, 64, 128)
        log_term(0, 2, "calc2")
        difference(diff0[:, 1, :], 0, 1, 0, M)
        bf11 = new_bf(1, 1, "log01")
        bf21 = new_bf(2, 1, "h01")
        cast_w1(nc.scalar.copy, bf11, 1, 1, 0, 64)
        cast_w1(nc.scalar.copy, bf21, 2, 1, 0, 64)
        quant_w1(0, 1, bf01, WHOLE)
        cast_w1(nc.vector.tensor_copy, bf11, 1, 1, 64, 128)
        cast_w1(nc.vector.tensor_copy, bf21, 2, 1, 64, 128)
        log_term(0, 3, "calc3")
        difference(diff0[:, 2, :], 0, 2, 0, M)
        quant_w1(1, 1, bf11, WHOLE)
        quant_w1(2, 1, bf21, FIRST_APART)
        difference(diff0[:, 3, :], 0, 3, 0, M)
        for t in range(4):
            for a in range(KP):
                stage1_pass(a, 1, t)
        mix_v = mix.rearrange("(i p) m -> p i m", p=P)
        mix_a = keep.tile([P, 4, M], F32, name="mix_a", tag="tab1", align_bytes=64)
        nc.sync.dma_start(out=mix_a[:], in_=mix_v[:, 0:4, :])
        mix_b = keep.tile([P, 2, M], F32, name="mix_b", tag="scales", align_bytes=64)
        nc.sync.dma_start(out=mix_b[:], in_=mix_v[:, 4:6, :])
        mix_pairs = [mix_a[:, 0:2, :], mix_a[:, 2:4, :], mix_b[:]]
        w4_w = keep.tile([P, HP, 2 * N], U8, name="w4_w", tag="raw0", align_bytes=64)
        nc.sync.dma_start(out=w4_w[:].bitcast(I32), in_=w4_words.rearrange("a p c -> p a c").bitcast(I32))
        w4_s = keep.tile([P, HP, N], U8, name="w4_s", tag="bf2", align_bytes=64)
        nc.gpsimd.memset(w4_s[:].rearrange("p a c -> p (a c)").bitcast(I32), 0)
        for q in range(4):
            nc.sync.dma_start(
                out=w4_s[32 * q : 32 * q + 4, :, :].bitcast(I32),
                in_=w4_scales[:, 4 * q : 4 * q + 4, :].rearrange("a r c -> r a c").bitcast(I32),
            )
        z0a_bf = scale_z(diff0[:, :, 0:HM], 0, HM, "0a", "h01")
        z0b_rows = keep.tile([P, 4, HM], BF16, name="z0b_rows", align_bytes=64)
        z0b_bf = keep.tile([P, HM, 4], BF16, name="z0b_bf", align_bytes=64)

        diff1 = keep.tile([P, 6, HM], F32, name="diff1")
        first = (2, 0)

        def difference1(half, t):
            difference(diff1[:, first[half] + t, :], 1, t, half * HM, (half + 1) * HM)

        evacuate(1, 0, nc.scalar.copy)
        evacuate(1, 1, nc.scalar.copy)
        evacuate(1, 2, nc.scalar.copy)
        log_term(1, 0, "calc0")
        z0a = quant_z(z0a_bf, HM, "0a")
        evacuate(1, 3, nc.scalar.copy)
        log_term(1, 1, "calc1")
        difference1(0, 0)
        difference1(1, 0)
        log_term(1, 2, "calc2")
        difference1(0, 1)
        difference1(1, 1)
        log_term(1, 3, "calc3")
        for t in range(4):
            nc.scalar.activation(z0b_rows[:, t, :], diff0[:, t, HM:M], ACT.Copy, scale=ngain[:, 0, t : t + 1])
        for m0 in (0, HM // 2):
            nc.scalar.copy(
                z0b_bf[:, m0 : m0 + HM // 2, :].rearrange("p (c i) t -> p c t i", i=4),
                z0b_rows[:, :, m0 : m0 + HM // 2].rearrange("p t (c i) -> p c t i", i=4),
            )
        difference1(0, 2)
        difference1(0, 3)

        out_v = out.rearrange("(i p) m -> p i m", p=P)
        ys = {}

        def stage2(half, z):
            for pair in range(N // P // 2):
                y = psum.tile([P, 2, HM], F32, name="bank%d%d" % (pair, half))
                ys[(half, pair)] = y
                for i in range(2):
                    n0 = (2 * pair + i) * P
                    for b in range(HP):
                        nc.tensor.matmul_mx(
                            out=y[:, i, :],
                            lhsT=w4_w[:, b, 2 * n0 : 2 * (n0 + P)].bitcast(FP4X4),
                            lhsT_scale=w4_s[:, b, n0 : n0 + P],
                            rhs=z[b][0][:].bitcast(FP8X4),
                            rhs_scale=z[b][1][:],
                            start=(b == 0),
                            stop=(b == HP - 1),
                        )

        def finish(half, pair):
            m0 = half * HM
            act = ring.tile([P, 2, HM], F32, name="act")
            nc.scalar.activation(act[:], ys[(half, pair)][:], ACT.Silu)
            res = keep.tile([P, 2, HM], F32, name="res%d%d" % (half, pair))
            nc.vector.tensor_tensor(res[:], act[:], mix_pairs[pair][:, :, m0 : m0 + HM], ALU.mult)
            nc.sync.dma_start(out=out_v[:, 2 * pair : 2 * pair + 2, m0 : m0 + HM], in_=res[:])

        za_bf = scale_z(diff1[:, 2:6, :], 1, HM, "1a", "z1a")
        difference1(1, 2)
        stage2(0, (z0a, quant_z(za_bf, HM, "1a")))
        difference1(1, 3)
        zb_bf = scale_z(diff1[:, 0:4, :], 1, HM, "1b", "z1b")
        z0b = quant_z(z0b_bf, HM, "0b")
        finish(0, 0)
        stage2(1, (z0b, quant_z(zb_bf, HM, "1b")))
        finish(0, 1)
        finish(0, 2)
        for pair in range(N // P // 2):
            finish(1, pair)
